import numpy as np
import ml_dtypes


def mxq(x, axis, fmt="e4m3"):
    dtype, down = {"e4m3": (ml_dtypes.float8_e4m3fn, 7), "e5m2": (ml_dtypes.float8_e5m2, 14)}[fmt]
    v = np.moveaxis(np.asarray(x, np.float32).astype(ml_dtypes.bfloat16).astype(np.float64), axis, -1)
    blocks = v.reshape(v.shape[:-1] + (-1, 32))
    amax = np.abs(blocks).max(-1, keepdims=True)
    byte = np.maximum(np.where(amax > 0, np.frexp(amax)[1] - 1 + 127, 0) - down, 1)
    scale = np.exp2(byte - 127.0)
    codes = (blocks / scale).astype(np.float32).astype(dtype).astype(np.float64)
    return np.moveaxis((codes * scale).reshape(v.shape), -1, axis)


WIDE = False


def mx_kscale(k):
    if not WIDE:
        return np.ones(k)
    levels = np.array([10, -10, 5, -5, 0])
    if k % 512:
        return np.exp2(np.random.permutation(np.resize(levels, k // 32))).repeat(32)
    a = np.empty((k // 512, 16))
    for p in range(k // 512):
        a[p, :8] = np.random.permutation(np.resize(levels, 8))
        for g in range(8):
            far = levels[np.abs(levels - a[p, g]) >= 10]
            a[p, g + 8] = far[np.random.randint(len(far))]
    return np.exp2(a.ravel()).repeat(32)


def f64(x):
    return np.asarray(x).astype(np.float64)


def striped(idx):
    return np.tile(idx.reshape(-1, 16).T, (8, 1)).astype(np.uint16)


def unstriped(offs):
    return offs[:16].T.reshape(-1).astype(np.int64)


def gelu(v):
    return 0.5 * v * (1.0 + np.tanh(np.sqrt(2.0 / np.pi) * (v + 0.044715 * v**3)))


K, T, E, C, H, N = 512, 640, 4, 256, 512, 128
PAD = 32


def by_expert(wq, xq):
    return np.concatenate([wq[e].T @ xq[:, e * C:(e + 1) * C] for e in range(E)], axis=1)


def setup_inputs():
    n = np.random.standard_normal
    s = mx_kscale(K)[:, None]
    u = mx_kscale(H)
    first = np.random.permutation(np.repeat(np.arange(E), T // E))
    second = (first + 1 + np.random.permutation(np.repeat(np.arange(E - 1), -(-T // (E - 1)))[:T])) % E
    while np.bincount(second, minlength=E).max() != T // E:
        load = np.bincount(second, minlength=E); hi, lo = int(load.argmax()), int(load.argmin())
        t = np.flatnonzero((second == hi) & (first != lo))[0]; second[t] = lo
    slot_token = np.empty(E * C, np.int64); pos = np.empty((2, T), np.int64); fill = np.zeros(E, np.int64)
    place = np.stack([np.random.permutation(C) for _ in range(E)])
    for r, deal in enumerate((first, second)):
        for t in np.random.permutation(T):
            e = deal[t]
            if fill[e] < C: j = e * C + place[e, fill[e]]; fill[e] += 1; slot_token[j] = t; pos[r, t] = j
            else: pos[r, t] = E * C + t % PAD
    g = np.random.uniform(0.2, 0.8, T)
    return {
        "xT": (n((K, T)) * s).astype(np.float32),
        "w1": (n((E, K, H)) / np.sqrt(K) / s[None]).astype(np.float32),
        "w3": (n((E, K, H)) / np.sqrt(K) / s[None] * u[None, None, :]).astype(np.float32),
        "w2": (n((E, H, N)) / np.sqrt(H) / u[None, :, None]).astype(np.float32),
        "gate": np.stack([np.tile(g, (N, 1)), np.tile(1.0 - g, (N, 1))]).astype(np.float32),
        "offs": striped(slot_token),
        "pos1": striped(pos[0]),
        "pos2": striped(pos[1]),
    }


def reference(xT, w1, w3, w2, gate, offs, pos1, pos2):
    idx = unstriped(offs)
    xq = mxq(f64(xT)[:, idx], 0, "e4m3")
    h = gelu(by_expert(mxq(f64(w1), 1, "e4m3"), xq))
    h = h * by_expert(mxq(f64(w3), 1, "e4m3"), xq)
    y = by_expert(mxq(f64(w2), 1, "e4m3"), mxq(h, 0, "e4m3"))
    y = np.concatenate([y, np.zeros((N, PAD))], axis=1)
    return f64(gate[0]) * y[:, unstriped(pos1)] + f64(gate[1]) * y[:, unstriped(pos2)]

@@ -1,0 +1,187 @@
+from contextlib import ExitStack
+
+import concourse.mybir as mybir
+
+F32 = mybir.dt.float32
+BF16 = mybir.dt.bfloat16
+U32 = mybir.dt.uint32
+U16 = mybir.dt.uint16
+U8 = mybir.dt.uint8
+FP8X4 = mybir.dt.float8_e4m3fn_x4
+MULT = mybir.AluOpType.mult
+ADD = mybir.AluOpType.add
+GELU = mybir.ActivationFunctionType.Gelu_apprx_tanh
+
+P = 128
+K, T, E, C, H, N = 512, 640, 4, 256, 512, 128
+S = E * C
+PAD = 32
+FLOPS = 2 * S * K * H * 2 + 2 * S * H * N
+MS1 = (88, 88, 72, 72)
+MS3 = (88, 88, 80, 96)
+W2_ENGINE = "SVVV"
+XCH = ((256, 256), (256, 192), (128, 0))
+
+
+def tile_moe_cap2_glu_gelu_kernel(tc, xT, w1, w3, w2, gate, offs, pos1, pos2, out):
+    nc = tc.nc
+    with ExitStack() as ctx:
+        lists = ctx.enter_context(tc.tile_pool(name="lists", bufs=1))
+        keep = ctx.enter_context(tc.tile_pool(name="keep", bufs=1))
+        raws = ctx.enter_context(tc.tile_pool(name="raws", bufs=4))
+        work = ctx.enter_context(tc.tile_pool(name="work", bufs=4))
+        psum = ctx.enter_context(tc.psum_pool(name="psum", bufs=3))
+        psum_y = ctx.enter_context(tc.psum_pool(name="psum_y", bufs=2))
+
+        offs_t = lists.tile([P, S // 16], U16, name="offs_t")
+        pos1_t = lists.tile([P, T // 16], U16, name="pos1_t")
+        pos2_t = lists.tile([P, T // 16], U16, name="pos2_t")
+
+        xv = xT.rearrange("(p j) t -> p j t", j=4)
+        xr = []
+        lo = 0
+        for width, s_cols in XCH:
+            xc = keep.tile([P, 4, width], F32, name=f"x{lo}")
+            nc.sync.dma_start(xc[:], xv[:, :, lo : lo + width])
+            xr.append(xc)
+            lo += width
+        nc.sync.dma_start(offs_t[:], offs)
+        r1, r3, r2 = [], [], []
+        gate_t = keep.tile([P, 2, T], F32, name="gate_t")
+        for e in range(E):
+            a = raws.tile([P, 4, H], F32, name="r1")
+            nc.sync.dma_start(a[:], w1[e].rearrange("(p j) i -> p j i", j=4))
+            b = raws.tile([P, 4, H], F32, name="r3")
+            nc.sync.dma_start(b[:], w3[e].rearrange("(p j) i -> p j i", j=4))
+            r1.append(a)
+            r3.append(b)
+        for e in range(E):
+            c = raws.tile([P, 4, N], F32, name="r2")
+            nc.sync.dma_start(c[:], w2[e].rearrange("(p j) n -> p j n", j=4))
+            r2.append(c)
+        nc.sync.dma_start(pos1_t[:], pos1)
+        nc.sync.dma_start(pos2_t[:], pos2)
+        nc.sync.dma_start(gate_t[:], gate.rearrange("c p t -> p c t"))
+
+        xs = keep.tile([P, T], U8, name="xs", align_bytes=64)
+        nc.gpsimd.memset(xs[:], 0)
+        ys = keep.tile([P, S + PAD], F32, name="ys")
+        nc.vector.memset(ys[:, S : S + PAD], 0.0)
+        dummy = keep.tile([P, 1], F32, name="dummy")
+        nc.vector.memset(dummy[:], 0.0)
+        dummy2 = keep.tile([P, 1], F32, name="dummy2")
+        nc.scalar.activation(out=dummy2[:], in_=dummy[:], func=GELU)
+
+        xb = keep.tile([P, T, 4], BF16, name="xb", align_bytes=64)
+        xq = keep.tile([P, T], U32, name="xq", align_bytes=64)
+
+        def turn(engine_copy, dst, src):
+            engine_copy(
+                out=dst.rearrange("p (c i) j -> p c j i", i=4),
+                in_=src.rearrange("p j (c i) -> p c j i", i=4),
+            )
+
+        lo = 0
+        for (width, s_cols), xc in zip(XCH, xr):
+            if s_cols:
+                turn(nc.scalar.copy, xb[:, lo : lo + s_cols, :], xc[:, :, 0:s_cols])
+            if s_cols < width:
+                turn(nc.vector.tensor_copy, xb[:, lo + s_cols : lo + width, :], xc[:, :, s_cols:width])
+            nc.vector.quantize_mx(
+                out=xq[:, lo : lo + width].bitcast(FP8X4),
+                scales=xs[:, lo : lo + width],
+                in_=xb[:, lo : lo + width, :].rearrange("p t j -> p (t j)"),
+            )
+            lo += width
+
+        def prepare(raw, tag, ms):
+            wb = work.tile([P, 4, P, 4], BF16, name=tag + "b", align_bytes=64)
+            wq = work.tile([P, H], U32, name=tag + "q", align_bytes=64)
+            ws = work.tile([P, H], U8, name=tag + "s", align_bytes=64)
+            for copy, lo, hi in ((nc.scalar.copy, 0, ms), (nc.vector.tensor_copy, ms, P)):
+                copy(
+                    out=wb[:, :, lo:hi, :].rearrange("p t m j -> p m j t"),
+                    in_=raw[:, :, 4 * lo : 4 * hi].rearrange("p j (m t) -> p m j t", t=4),
+                )
+            nc.vector.quantize_mx(out=wq[:].bitcast(FP8X4), scales=ws[:], in_=wb[:].rearrange("p t m j -> p (t m j)"))
+            return wq, ws
+
+        for e in range(E):
+            xgw = work.tile([P, C], U32, name="xgw", align_bytes=64)
+            xgs = work.tile([P, C], U8, name="xgs", align_bytes=64)
+            cols = slice(e * C // 16, (e + 1) * C // 16)
+            nc.vector.tensor_copy(xgw[:], xq[:].indirect(offs_t[:, cols]))
+            nc.vector.tensor_copy(xgs[:], xs[:].indirect(offs_t[:, cols]))
+
+            def project(wq, ws, tag):
+                banks = []
+                for half in range(2):
+                    acc = psum.tile([P, 4, P], F32, name=tag)
+                    sl = slice(half * P, (half + 1) * P)
+                    for t in range(4):
+                        tl = slice(t * P, (t + 1) * P)
+                        nc.tensor.matmul_mx(
+                            out=acc[:, t, :],
+                            lhsT=wq[:, tl].bitcast(FP8X4),
+                            lhsT_scale=ws[:, tl],
+                            rhs=xgw[:, sl].bitcast(FP8X4),
+                            rhs_scale=xgs[:, sl],
+                            start=True,
+                            stop=True,
+                        )
+                    banks.append(acc)
+                return banks
+
+            w1q, w1s = prepare(r1[e], "w1", MS1[e])
+            banks_a = project(w1q, w1s, "acc_a")
+            gs = []
+            for half in range(2):
+                g = work.tile([P, P, 4], F32, name="g")
+                nc.scalar.activation(out=g[:], in_=banks_a[half][:].rearrange("p t n -> p n t"), func=GELU)
+                gs.append(g)
+            w3q, w3s = prepare(r3[e], "w3", MS3[e])
+            banks_b = project(w3q, w3s, "acc_b")
+
+            w2b = work.tile([P, N, 4], BF16, name="w2b", align_bytes=64)
+            w2q = work.tile([P, N], U32, name="w2q", align_bytes=64)
+            w2s = work.tile([P, N], U8, name="w2s", align_bytes=64)
+            turn(nc.scalar.copy if W2_ENGINE[e] == "S" else nc.vector.tensor_copy, w2b[:], r2[e][:])
+
+            hb = work.tile([P, C, 4], BF16, name="hb", align_bytes=64)
+            hq = work.tile([P, C], U32, name="hq", align_bytes=64)
+            hs = work.tile([P, C], U8, name="hs", align_bytes=64)
+            for half in range(2):
+                sl = slice(half * P, (half + 1) * P)
+                nc.vector.tensor_tensor(
+                    out=hb[:, sl, :], in0=gs[half][:], in1=banks_b[half][:].rearrange("p t n -> p n t"), op=MULT
+                )
+            nc.vector.quantize_mx(out=w2q[:].bitcast(FP8X4), scales=w2s[:], in_=w2b[:].rearrange("p n j -> p (n j)"))
+            y = psum_y.tile([P, C], F32, name="y")
+            pieces = (slice(0, P), slice(P, C)) if e == E - 1 else (slice(0, C),)
+            for sl in pieces:
+                nc.vector.quantize_mx(
+                    out=hq[:, sl].bitcast(FP8X4), scales=hs[:, sl], in_=hb[:, sl, :].rearrange("p n j -> p (n j)")
+                )
+            for sl in pieces:
+                nc.tensor.matmul_mx(
+                    out=y[:, sl],
+                    lhsT=w2q[:].bitcast(FP8X4),
+                    lhsT_scale=w2s[:],
+                    rhs=hq[:, sl].bitcast(FP8X4),
+                    rhs_scale=hs[:, sl],
+                    start=True,
+                    stop=True,
+                )
+            nc.scalar.copy(out=ys[:, e * C : (e + 1) * C], in_=y[:])
+
+        half_t = T // 2
+        for i in range(2):
+            cols = slice(i * half_t // 16, (i + 1) * half_t // 16)
+            toks = slice(i * half_t, (i + 1) * half_t)
+            z1 = work.tile([P, half_t], F32, name="z1")
+            z2 = work.tile([P, half_t], F32, name="z2")
+            z = work.tile([P, half_t], F32, name="z")
+            nc.vector.tensor_tensor(z1[:], ys[:].indirect(pos1_t[:, cols]), gate_t[:, 0, toks], MULT)
+            nc.vector.tensor_tensor(z2[:], ys[:].indirect(pos2_t[:, cols]), gate_t[:, 1, toks], MULT)
+            nc.vector.tensor_tensor(z[:], z1[:], z2[:], ADD)
+            nc.sync.dma_start(out[:, toks], z[:])

@@ -4,6 +4,7 @@ import concourse.mybir as mybir
 
 F32 = mybir.dt.float32
 BF16 = mybir.dt.bfloat16
+I32 = mybir.dt.int32
 U32 = mybir.dt.uint32
 U16 = mybir.dt.uint16
 U8 = mybir.dt.uint8
@@ -16,11 +17,16 @@ P = 128
 K, T, E, C, H, N = 512, 640, 4, 256, 512, 128
 S = E * C
 PAD = 32
+WIN = 704
 FLOPS = 2 * S * K * H * 2 + 2 * S * H * N
-MS1 = (88, 88, 72, 72)
-MS3 = (88, 88, 80, 96)
-W2_ENGINE = "SVVV"
-XCH = ((256, 256), (256, 192), (128, 0))
+MS1 = (128, 72, 72, 64)
+MS3 = (72, 72, 72, 72)
+W2S = (1, 2)
+W2_LOAD = (3, 3)
+W2_AT = (3, 3)
+Y_GROUPS = ((0, 1), (2,), (3,))
+Y_AT = {(0, 1): 3, (2,): 3, (3,): 3}
+XCH = ((256, 0), (256, 128), (128, 0))
 
 
 def tile_moe_cap2_glu_gelu_kernel(tc, xT, w1, w3, w2, gate, offs, pos1, pos2, out):
@@ -28,7 +34,6 @@ def tile_moe_cap2_glu_gelu_kernel(tc, xT, w1, w3, w2, gate, offs, pos1, pos2, ou
     with ExitStack() as ctx:
         lists = ctx.enter_context(tc.tile_pool(name="lists", bufs=1))
         keep = ctx.enter_context(tc.tile_pool(name="keep", bufs=1))
-        raws = ctx.enter_context(tc.tile_pool(name="raws", bufs=4))
         work = ctx.enter_context(tc.tile_pool(name="work", bufs=4))
         psum = ctx.enter_context(tc.psum_pool(name="psum", bufs=3))
         psum_y = ctx.enter_context(tc.psum_pool(name="psum_y", bufs=2))
@@ -48,23 +53,31 @@ def tile_moe_cap2_glu_gelu_kernel(tc, xT, w1, w3, w2, gate, offs, pos1, pos2, ou
         nc.sync.dma_start(offs_t[:], offs)
         r1, r3, r2 = [], [], []
         gate_t = keep.tile([P, 2, T], F32, name="gate_t")
+        w2v = w2.rearrange("e (p j) n -> p e j n", j=4)
+
+        def load_w2(pair):
+            c = keep.tile([P, 2, 4, N], F32, name=f"r2_{pair}")
+            nc.sync.dma_start(c[:], w2v[:, 2 * pair : 2 * pair + 2])
+            r2.append(c)
+
         for e in range(E):
-            a = raws.tile([P, 4, H], F32, name="r1")
+            a = keep.tile([P, 4, H], F32, name=f"r1_{e}")
             nc.sync.dma_start(a[:], w1[e].rearrange("(p j) i -> p j i", j=4))
-            b = raws.tile([P, 4, H], F32, name="r3")
+            b = keep.tile([P, 4, H], F32, name=f"r3_{e}")
             nc.sync.dma_start(b[:], w3[e].rearrange("(p j) i -> p j i", j=4))
             r1.append(a)
             r3.append(b)
-        for e in range(E):
-            c = raws.tile([P, 4, N], F32, name="r2")
-            nc.sync.dma_start(c[:], w2[e].rearrange("(p j) n -> p j n", j=4))
-            r2.append(c)
+            for pair in range(2):
+                if W2_LOAD[pair] == e:
+                    load_w2(pair)
         nc.sync.dma_start(pos1_t[:], pos1)
         nc.sync.dma_start(pos2_t[:], pos2)
         nc.sync.dma_start(gate_t[:], gate.rearrange("c p t -> p c t"))
 
-        xs = keep.tile([P, T], U8, name="xs", align_bytes=64)
+        xs = keep.tile([P, WIN], U8, name="xs", align_bytes=64)
         nc.gpsimd.memset(xs[:], 0)
+        xq = keep.tile([P, WIN], I32, name="xq", align_bytes=64)
+        nc.vector.memset(xq[:, T:WIN], 0)
         ys = keep.tile([P, S + PAD], F32, name="ys")
         nc.vector.memset(ys[:, S : S + PAD], 0.0)
         dummy = keep.tile([P, 1], F32, name="dummy")
@@ -73,7 +86,6 @@ def tile_moe_cap2_glu_gelu_kernel(tc, xT, w1, w3, w2, gate, offs, pos1, pos2, ou
         nc.scalar.activation(out=dummy2[:], in_=dummy[:], func=GELU)
 
         xb = keep.tile([P, T, 4], BF16, name="xb", align_bytes=64)
-        xq = keep.tile([P, T], U32, name="xq", align_bytes=64)
 
         def turn(engine_copy, dst, src):
             engine_copy(
@@ -99,89 +111,120 @@ def tile_moe_cap2_glu_gelu_kernel(tc, xT, w1, w3, w2, gate, offs, pos1, pos2, ou
             wq = work.tile([P, H], U32, name=tag + "q", align_bytes=64)
             ws = work.tile([P, H], U8, name=tag + "s", align_bytes=64)
             for copy, lo, hi in ((nc.scalar.copy, 0, ms), (nc.vector.tensor_copy, ms, P)):
-                copy(
-                    out=wb[:, :, lo:hi, :].rearrange("p t m j -> p m j t"),
-                    in_=raw[:, :, 4 * lo : 4 * hi].rearrange("p j (m t) -> p m j t", t=4),
-                )
+                if lo < hi:
+                    copy(
+                        out=wb[:, :, lo:hi, :].rearrange("p (u v) m j -> p u m j v", v=2),
+                        in_=raw[:, :, 4 * lo : 4 * hi].rearrange("p j (m u v) -> p u m j v", u=2, v=2),
+                    )
             nc.vector.quantize_mx(out=wq[:].bitcast(FP8X4), scales=ws[:], in_=wb[:].rearrange("p t m j -> p (t m j)"))
             return wq, ws
 
-        for e in range(E):
-            xgw = work.tile([P, C], U32, name="xgw", align_bytes=64)
-            xgs = work.tile([P, C], U8, name="xgs", align_bytes=64)
-            cols = slice(e * C // 16, (e + 1) * C // 16)
-            nc.vector.tensor_copy(xgw[:], xq[:].indirect(offs_t[:, cols]))
+        def gather(e, count):
+            xgw = work.tile([P, count * C], U32, name="xgw", align_bytes=64)
+            xgs = work.tile([P, count * C], U8, name="xgs", align_bytes=64)
+            cols = slice(e * C // 16, (e + count) * C // 16)
+            nc.vector.tensor_copy(xgw[:], xq[:].bitcast(U32).indirect(offs_t[:, cols]))
             nc.vector.tensor_copy(xgs[:], xs[:].indirect(offs_t[:, cols]))
+            return [(xgw[:, i * C : (i + 1) * C], xgs[:, i * C : (i + 1) * C]) for i in range(count)]
 
-            def project(wq, ws, tag):
-                banks = []
-                for half in range(2):
-                    acc = psum.tile([P, 4, P], F32, name=tag)
-                    sl = slice(half * P, (half + 1) * P)
-                    for t in range(4):
-                        tl = slice(t * P, (t + 1) * P)
-                        nc.tensor.matmul_mx(
-                            out=acc[:, t, :],
-                            lhsT=wq[:, tl].bitcast(FP8X4),
-                            lhsT_scale=ws[:, tl],
-                            rhs=xgw[:, sl].bitcast(FP8X4),
-                            rhs_scale=xgs[:, sl],
-                            start=True,
-                            stop=True,
-                        )
-                    banks.append(acc)
-                return banks
-
-            w1q, w1s = prepare(r1[e], "w1", MS1[e])
-            banks_a = project(w1q, w1s, "acc_a")
-            gs = []
+        def project(weights, tokens, tag):
+            wq, ws = weights
+            xgw, xgs = tokens
+            banks = []
             for half in range(2):
-                g = work.tile([P, P, 4], F32, name="g")
-                nc.scalar.activation(out=g[:], in_=banks_a[half][:].rearrange("p t n -> p n t"), func=GELU)
-                gs.append(g)
-            w3q, w3s = prepare(r3[e], "w3", MS3[e])
-            banks_b = project(w3q, w3s, "acc_b")
-
-            w2b = work.tile([P, N, 4], BF16, name="w2b", align_bytes=64)
-            w2q = work.tile([P, N], U32, name="w2q", align_bytes=64)
-            w2s = work.tile([P, N], U8, name="w2s", align_bytes=64)
-            turn(nc.scalar.copy if W2_ENGINE[e] == "S" else nc.vector.tensor_copy, w2b[:], r2[e][:])
-
-            hb = work.tile([P, C, 4], BF16, name="hb", align_bytes=64)
-            hq = work.tile([P, C], U32, name="hq", align_bytes=64)
-            hs = work.tile([P, C], U8, name="hs", align_bytes=64)
-            for half in range(2):
+                acc = psum.tile([P, 4, P], F32, name=tag)
                 sl = slice(half * P, (half + 1) * P)
-                nc.vector.tensor_tensor(
-                    out=hb[:, sl, :], in0=gs[half][:], in1=banks_b[half][:].rearrange("p t n -> p n t"), op=MULT
-                )
-            nc.vector.quantize_mx(out=w2q[:].bitcast(FP8X4), scales=w2s[:], in_=w2b[:].rearrange("p n j -> p (n j)"))
-            y = psum_y.tile([P, C], F32, name="y")
-            pieces = (slice(0, P), slice(P, C)) if e == E - 1 else (slice(0, C),)
-            for sl in pieces:
-                nc.vector.quantize_mx(
-                    out=hq[:, sl].bitcast(FP8X4), scales=hs[:, sl], in_=hb[:, sl, :].rearrange("p n j -> p (n j)")
-                )
+                for t in range(4):
+                    tl = slice(t * P, (t + 1) * P)
+                    nc.tensor.matmul_mx(
+                        out=acc[:, t, :],
+                        lhsT=wq[:, tl].bitcast(FP8X4),
+                        lhsT_scale=ws[:, tl],
+                        rhs=xgw[:, sl].bitcast(FP8X4),
+                        rhs_scale=xgs[:, sl],
+                        start=True,
+                        stop=True,
+                    )
+                banks.append(acc)
+            return banks
+
+        def prepare_w2(pair):
+            w2b = work.tile([P, 2, N, 4], BF16, name="w2b", align_bytes=64)
+            w2q = work.tile([P, 2 * N], U32, name="w2q", align_bytes=64)
+            w2s = work.tile([P, 2 * N], U8, name="w2s", align_bytes=64)
+            for i in range(2):
+                turn(nc.scalar.copy if i < W2S[pair] else nc.vector.tensor_copy, w2b[:, i], r2[pair][:, i])
+            nc.vector.quantize_mx(
+                out=w2q[:].bitcast(FP8X4), scales=w2s[:], in_=w2b[:].rearrange("p e n j -> p (e n j)")
+            )
+            return [(w2q[:, i * N : (i + 1) * N], w2s[:, i * N : (i + 1) * N]) for i in range(2)]
+
+        def finish(acc, weights, hidden, pieces):
+            w2q, w2s = weights
+            hq, hs = hidden
             for sl in pieces:
                 nc.tensor.matmul_mx(
-                    out=y[:, sl],
-                    lhsT=w2q[:].bitcast(FP8X4),
-                    lhsT_scale=w2s[:],
+                    out=acc[:, sl],
+                    lhsT=w2q.bitcast(FP8X4),
+                    lhsT_scale=w2s,
                     rhs=hq[:, sl].bitcast(FP8X4),
                     rhs_scale=hs[:, sl],
                     start=True,
                     stop=True,
                 )
-            nc.scalar.copy(out=ys[:, e * C : (e + 1) * C], in_=y[:])
 
-        half_t = T // 2
+        halves = (slice(0, P), slice(P, C))
+        whole = (slice(0, C),)
+        hidden = []
+        w2qs = {}
+        tokens = {}
+        tokens[0], tokens[1] = gather(0, 2)
+        for e in range(E):
+            if e == 1:
+                tokens[2], tokens[3] = gather(2, 2)
+            banks_a = project(prepare(r1[e], "w1", MS1[e]), tokens[e], "acc_a")
+            w3qs = prepare(r3[e], "w3", MS3[e])
+            gs = []
+            for half in range(2):
+                g = work.tile([P, P, 4], F32, name="g")
+                nc.scalar.activation(out=g[:], in_=banks_a[half][:].rearrange("p t n -> p n t"), func=GELU)
+                gs.append(g)
+            banks_b = project(w3qs, tokens[e], "acc_b")
+            for pair in range(2):
+                if W2_AT[pair] == e:
+                    w2qs[2 * pair], w2qs[2 * pair + 1] = prepare_w2(pair)
+            hb = work.tile([P, C, 4], BF16, name="hb", align_bytes=64)
+            hq = work.tile([P, C], U32, name="hq", align_bytes=64)
+            hs = work.tile([P, C], U8, name="hs", align_bytes=64)
+            for half in range(2):
+                nc.vector.tensor_tensor(
+                    out=hb[:, halves[half], :], in0=gs[half][:], in1=banks_b[half][:].rearrange("p t n -> p n t"), op=MULT
+                )
+            pieces = halves if e == E - 1 else whole
+            for sl in pieces:
+                nc.vector.quantize_mx(
+                    out=hq[:, sl].bitcast(FP8X4), scales=hs[:, sl], in_=hb[:, sl, :].rearrange("p n j -> p (n j)")
+                )
+            hidden.append((hq, hs))
+            for group in Y_GROUPS:
+                if e == Y_AT[group]:
+                    y = psum_y.tile([P, 2 * C], F32, name="y")
+                    for i, f in enumerate(group):
+                        finish(y[:, i * C : (i + 1) * C], w2qs[f], hidden[f], halves if f == E - 1 else whole)
+                    lo = group[0] * C
+                    hi = lo + len(group) * C
+                    nc.scalar.copy(out=ys[:, lo:hi], in_=y[:, 0 : hi - lo])
+
+        cuts = (0, 448, T)
+        toks = [slice(cuts[i], cuts[i + 1]) for i in range(2)]
+        z1 = keep.tile([P, T], F32, name="z1")
+        nc.vector.tensor_tensor(z1[:], ys[:].indirect(pos1_t[:]), gate_t[:, 0, :], MULT)
+        z2 = []
         for i in range(2):
-            cols = slice(i * half_t // 16, (i + 1) * half_t // 16)
-            toks = slice(i * half_t, (i + 1) * half_t)
-            z1 = work.tile([P, half_t], F32, name="z1")
-            z2 = work.tile([P, half_t], F32, name="z2")
-            z = work.tile([P, half_t], F32, name="z")
-            nc.vector.tensor_tensor(z1[:], ys[:].indirect(pos1_t[:, cols]), gate_t[:, 0, toks], MULT)
-            nc.vector.tensor_tensor(z2[:], ys[:].indirect(pos2_t[:, cols]), gate_t[:, 1, toks], MULT)
-            nc.vector.tensor_tensor(z[:], z1[:], z2[:], ADD)
-            nc.sync.dma_start(out[:, toks], z[:])
+            z2.append(keep.tile([P, cuts[i + 1] - cuts[i]], F32, name=f"z2_{i}"))
+            cols = slice(cuts[i] // 16, cuts[i + 1] // 16)
+            nc.vector.tensor_tensor(z2[i][:], ys[:].indirect(pos2_t[:, cols]), gate_t[:, 1, toks[i]], MULT)
+        for i in range(2):
+            total = keep.tile([P, cuts[i + 1] - cuts[i]], F32, name=f"total{i}")
+            nc.vector.tensor_tensor(total[:], z1[:, toks[i]], z2[i][:], ADD)
+            nc.sync.dma_start(out[:, toks[i]], total[:])

@@ -19,8 +19,9 @@ S = E * C
 PAD = 32
 WIN = 704
 FLOPS = 2 * S * K * H * 2 + 2 * S * H * N
-MS1 = (128, 72, 72, 64)
-MS3 = (72, 72, 72, 72)
+MS1 = (128, 80, 80, 56)
+MS3 = ((80,), (80,), (80,), (40, 24))
+CUTS3 = (((0, P),), ((0, P),), ((0, P),), ((0, 64), (64, P)))
 W2S = (1, 2)
 W2_LOAD = (3, 3)
 W2_AT = (3, 3)
@@ -52,7 +53,7 @@ def tile_moe_cap2_glu_gelu_kernel(tc, xT, w1, w3, w2, gate, offs, pos1, pos2, ou
             lo += width
         nc.sync.dma_start(offs_t[:], offs)
         r1, r3, r2 = [], [], []
-        gate_t = keep.tile([P, 2, T], F32, name="gate_t")
+        gates = [keep.tile([P, T], F32, name=f"gate{c}") for c in range(2)]
         w2v = w2.rearrange("e (p j) n -> p e j n", j=4)
 
         def load_w2(pair):
@@ -63,16 +64,21 @@ def tile_moe_cap2_glu_gelu_kernel(tc, xT, w1, w3, w2, gate, offs, pos1, pos2, ou
         for e in range(E):
             a = keep.tile([P, 4, H], F32, name=f"r1_{e}")
             nc.sync.dma_start(a[:], w1[e].rearrange("(p j) i -> p j i", j=4))
-            b = keep.tile([P, 4, H], F32, name=f"r3_{e}")
-            nc.sync.dma_start(b[:], w3[e].rearrange("(p j) i -> p j i", j=4))
-            r1.append(a)
-            r3.append(b)
+            w3e = w3[e].rearrange("(p j) i -> p j i", j=4)
+            parts = []
+            for lo, hi in CUTS3[e]:
+                b = keep.tile([P, 4, 4 * (hi - lo)], F32, name=f"r3_{e}_{lo}")
+                nc.sync.dma_start(b[:], w3e[:, :, 4 * lo : 4 * hi])
+                parts.append(b)
+            r1.append([a])
+            r3.append(parts)
             for pair in range(2):
                 if W2_LOAD[pair] == e:
                     load_w2(pair)
         nc.sync.dma_start(pos1_t[:], pos1)
         nc.sync.dma_start(pos2_t[:], pos2)
-        nc.sync.dma_start(gate_t[:], gate.rearrange("c p t -> p c t"))
+        for c in range(2):
+            nc.sync.dma_start(gates[c][:], gate[c])
 
         xs = keep.tile([P, WIN], U8, name="xs", align_bytes=64)
         nc.gpsimd.memset(xs[:], 0)
@@ -106,17 +112,30 @@ def tile_moe_cap2_glu_gelu_kernel(tc, xT, w1, w3, w2, gate, offs, pos1, pos2, ou
             )
             lo += width
 
-        def prepare(raw, tag, ms):
+        def prepare(raws, tag, cuts, shares):
             wb = work.tile([P, 4, P, 4], BF16, name=tag + "b", align_bytes=64)
-            wq = work.tile([P, H], U32, name=tag + "q", align_bytes=64)
-            ws = work.tile([P, H], U8, name=tag + "s", align_bytes=64)
-            for copy, lo, hi in ((nc.scalar.copy, 0, ms), (nc.vector.tensor_copy, ms, P)):
-                if lo < hi:
-                    copy(
-                        out=wb[:, :, lo:hi, :].rearrange("p (u v) m j -> p u m j v", v=2),
-                        in_=raw[:, :, 4 * lo : 4 * hi].rearrange("p j (m u v) -> p u m j v", u=2, v=2),
+            wq = work.tile([P, 4, P], U32, name=tag + "q", align_bytes=64)
+            ws = work.tile([P, 4, P], U8, name=tag + "s", align_bytes=64)
+            for raw, (lo, hi), share in zip(raws, cuts, shares):
+                for copy, c0, c1 in ((nc.scalar.copy, lo, lo + share), (nc.vector.tensor_copy, lo + share, hi)):
+                    if c0 < c1:
+                        copy(
+                            out=wb[:, :, c0:c1, :].rearrange("p (u v) m j -> p u m j v", v=2),
+                            in_=raw[:, :, 4 * (c0 - lo) : 4 * (c1 - lo)].rearrange("p j (m u v) -> p u m j v", u=2, v=2),
+                        )
+                if hi - lo == P:
+                    nc.vector.quantize_mx(
+                        out=wq[:].rearrange("p t m -> p (t m)").bitcast(FP8X4),
+                        scales=ws[:].rearrange("p t m -> p (t m)"),
+                        in_=wb[:].rearrange("p t m j -> p (t m j)"),
                     )
-            nc.vector.quantize_mx(out=wq[:].bitcast(FP8X4), scales=ws[:], in_=wb[:].rearrange("p t m j -> p (t m j)"))
+                else:
+                    for t in range(4):
+                        nc.vector.quantize_mx(
+                            out=wq[:, t, lo:hi].bitcast(FP8X4),
+                            scales=ws[:, t, lo:hi],
+                            in_=wb[:, t, lo:hi, :].rearrange("p m j -> p (m j)"),
+                        )
             return wq, ws
 
         def gather(e, count):
@@ -135,11 +154,10 @@ def tile_moe_cap2_glu_gelu_kernel(tc, xT, w1, w3, w2, gate, offs, pos1, pos2, ou
                 acc = psum.tile([P, 4, P], F32, name=tag)
                 sl = slice(half * P, (half + 1) * P)
                 for t in range(4):
-                    tl = slice(t * P, (t + 1) * P)
                     nc.tensor.matmul_mx(
                         out=acc[:, t, :],
-                        lhsT=wq[:, tl].bitcast(FP8X4),
-                        lhsT_scale=ws[:, tl],
+                        lhsT=wq[:, t, :].bitcast(FP8X4),
+                        lhsT_scale=ws[:, t, :],
                         rhs=xgw[:, sl].bitcast(FP8X4),
                         rhs_scale=xgs[:, sl],
                         start=True,
@@ -182,8 +200,8 @@ def tile_moe_cap2_glu_gelu_kernel(tc, xT, w1, w3, w2, gate, offs, pos1, pos2, ou
         for e in range(E):
             if e == 1:
                 tokens[2], tokens[3] = gather(2, 2)
-            banks_a = project(prepare(r1[e], "w1", MS1[e]), tokens[e], "acc_a")
-            w3qs = prepare(r3[e], "w3", MS3[e])
+            banks_a = project(prepare(r1[e], "w1", ((0, P),), (MS1[e],)), tokens[e], "acc_a")
+            w3qs = prepare(r3[e], "w3", CUTS3[e], MS3[e])
             gs = []
             for half in range(2):
                 g = work.tile([P, P, 4], F32, name="g")
@@ -213,17 +231,20 @@ def tile_moe_cap2_glu_gelu_kernel(tc, xT, w1, w3, w2, gate, offs, pos1, pos2, ou
                         finish(y[:, i * C : (i + 1) * C], w2qs[f], hidden[f], halves if f == E - 1 else whole)
                     lo = group[0] * C
                     hi = lo + len(group) * C
-                    nc.scalar.copy(out=ys[:, lo:hi], in_=y[:, 0 : hi - lo])
+                    cut = lo + P if e == E - 1 and group == (E - 1,) else hi
+                    nc.scalar.copy(out=ys[:, lo:cut], in_=y[:, 0 : cut - lo])
+                    if cut < hi:
+                        nc.scalar.copy(out=ys[:, cut:hi], in_=y[:, cut - lo : hi - lo])
 
         cuts = (0, 448, T)
         toks = [slice(cuts[i], cuts[i + 1]) for i in range(2)]
         z1 = keep.tile([P, T], F32, name="z1")
-        nc.vector.tensor_tensor(z1[:], ys[:].indirect(pos1_t[:]), gate_t[:, 0, :], MULT)
+        nc.vector.tensor_tensor(z1[:], ys[:].indirect(pos1_t[:]), gates[0][:], MULT)
         z2 = []
         for i in range(2):
             z2.append(keep.tile([P, cuts[i + 1] - cuts[i]], F32, name=f"z2_{i}"))
             cols = slice(cuts[i] // 16, cuts[i + 1] // 16)
-            nc.vector.tensor_tensor(z2[i][:], ys[:].indirect(pos2_t[:, cols]), gate_t[:, 1, toks[i]], MULT)
+            nc.vector.tensor_tensor(z2[i][:], ys[:].indirect(pos2_t[:, cols]), gates[1][:, toks[i]], MULT)
         for i in range(2):
             total = keep.tile([P, cuts[i + 1] - cuts[i]], F32, name=f"total{i}")
             nc.vector.tensor_tensor(total[:], z1[:, toks[i]], z2[i][:], ADD)

from contextlib import ExitStack

import concourse.mybir as mybir

F32 = mybir.dt.float32
BF16 = mybir.dt.bfloat16
I32 = mybir.dt.int32
U32 = mybir.dt.uint32
U16 = mybir.dt.uint16
U8 = mybir.dt.uint8
FP8X4 = mybir.dt.float8_e4m3fn_x4
MULT = mybir.AluOpType.mult
ADD = mybir.AluOpType.add
GELU = mybir.ActivationFunctionType.Gelu_apprx_tanh

P = 128
K, T, E, C, H, N = 512, 640, 4, 256, 512, 128
S = E * C
PAD = 32
WIN = 704
FLOPS = 2 * S * K * H * 2 + 2 * S * H * N
MS1 = (128, 80, 80, 56)
MS3 = ((80,), (80,), (80,), (40, 24))
CUTS3 = (((0, P),), ((0, P),), ((0, P),), ((0, 64), (64, P)))
W2S = (1, 2)
W2_LOAD = (3, 3)
W2_AT = (3, 3)
Y_GROUPS = ((0, 1), (2,), (3,))
Y_AT = {(0, 1): 3, (2,): 3, (3,): 3}
XCH = ((256, 0), (256, 128), (128, 0))


def tile_moe_cap2_glu_gelu_kernel(tc, xT, w1, w3, w2, gate, offs, pos1, pos2, out):
    nc = tc.nc
    with ExitStack() as ctx:
        lists = ctx.enter_context(tc.tile_pool(name="lists", bufs=1))
        keep = ctx.enter_context(tc.tile_pool(name="keep", bufs=1))
        work = ctx.enter_context(tc.tile_pool(name="work", bufs=4))
        psum = ctx.enter_context(tc.psum_pool(name="psum", bufs=3))
        psum_y = ctx.enter_context(tc.psum_pool(name="psum_y", bufs=2))

        offs_t = lists.tile([P, S // 16], U16, name="offs_t")
        pos1_t = lists.tile([P, T // 16], U16, name="pos1_t")
        pos2_t = lists.tile([P, T // 16], U16, name="pos2_t")

        xv = xT.rearrange("(p j) t -> p j t", j=4)
        xr = []
        lo = 0
        for width, s_cols in XCH:
            xc = keep.tile([P, 4, width], F32, name=f"x{lo}")
            nc.sync.dma_start(xc[:], xv[:, :, lo : lo + width])
            xr.append(xc)
            lo += width
        nc.sync.dma_start(offs_t[:], offs)
        r1, r3, r2 = [], [], []
        gates = [keep.tile([P, T], F32, name=f"gate{c}") for c in range(2)]
        w2v = w2.rearrange("e (p j) n -> p e j n", j=4)

        def load_w2(pair):
            c = keep.tile([P, 2, 4, N], F32, name=f"r2_{pair}")
            nc.sync.dma_start(c[:], w2v[:, 2 * pair : 2 * pair + 2])
            r2.append(c)

        for e in range(E):
            a = keep.tile([P, 4, H], F32, name=f"r1_{e}")
            nc.sync.dma_start(a[:], w1[e].rearrange("(p j) i -> p j i", j=4))
            w3e = w3[e].rearrange("(p j) i -> p j i", j=4)
            parts = []
            for lo, hi in CUTS3[e]:
                b = keep.tile([P, 4, 4 * (hi - lo)], F32, name=f"r3_{e}_{lo}")
                nc.sync.dma_start(b[:], w3e[:, :, 4 * lo : 4 * hi])
                parts.append(b)
            r1.append([a])
            r3.append(parts)
            for pair in range(2):
                if W2_LOAD[pair] == e:
                    load_w2(pair)
        nc.sync.dma_start(pos1_t[:], pos1)
        nc.sync.dma_start(pos2_t[:], pos2)
        for c in range(2):
            nc.sync.dma_start(gates[c][:], gate[c])

        xs = keep.tile([P, WIN], U8, name="xs", align_bytes=64)
        nc.gpsimd.memset(xs[:], 0)
        xq = keep.tile([P, WIN], I32, name="xq", align_bytes=64)
        nc.vector.memset(xq[:, T:WIN], 0)
        ys = keep.tile([P, S + PAD], F32, name="ys")
        nc.vector.memset(ys[:, S : S + PAD], 0.0)
        dummy = keep.tile([P, 1], F32, name="dummy")
        nc.vector.memset(dummy[:], 0.0)
        dummy2 = keep.tile([P, 1], F32, name="dummy2")
        nc.scalar.activation(out=dummy2[:], in_=dummy[:], func=GELU)

        xb = keep.tile([P, T, 4], BF16, name="xb", align_bytes=64)

        def turn(engine_copy, dst, src):
            engine_copy(
                out=dst.rearrange("p (c i) j -> p c j i", i=4),
                in_=src.rearrange("p j (c i) -> p c j i", i=4),
            )

        lo = 0
        for (width, s_cols), xc in zip(XCH, xr):
            if s_cols:
                turn(nc.scalar.copy, xb[:, lo : lo + s_cols, :], xc[:, :, 0:s_cols])
            if s_cols < width:
                turn(nc.vector.tensor_copy, xb[:, lo + s_cols : lo + width, :], xc[:, :, s_cols:width])
            nc.vector.quantize_mx(
                out=xq[:, lo : lo + width].bitcast(FP8X4),
                scales=xs[:, lo : lo + width],
                in_=xb[:, lo : lo + width, :].rearrange("p t j -> p (t j)"),
            )
            lo += width

        def prepare(raws, tag, cuts, shares):
            wb = work.tile([P, 4, P, 4], BF16, name=tag + "b", align_bytes=64)
            wq = work.tile([P, 4, P], U32, name=tag + "q", align_bytes=64)
            ws = work.tile([P, 4, P], U8, name=tag + "s", align_bytes=64)
            for raw, (lo, hi), share in zip(raws, cuts, shares):
                for copy, c0, c1 in ((nc.scalar.copy, lo, lo + share), (nc.vector.tensor_copy, lo + share, hi)):
                    if c0 < c1:
                        copy(
                            out=wb[:, :, c0:c1, :].rearrange("p (u v) m j -> p u m j v", v=2),
                            in_=raw[:, :, 4 * (c0 - lo) : 4 * (c1 - lo)].rearrange("p j (m u v) -> p u m j v", u=2, v=2),
                        )
                if hi - lo == P:
                    nc.vector.quantize_mx(
                        out=wq[:].rearrange("p t m -> p (t m)").bitcast(FP8X4),
                        scales=ws[:].rearrange("p t m -> p (t m)"),
                        in_=wb[:].rearrange("p t m j -> p (t m j)"),
                    )
                else:
                    for t in range(4):
                        nc.vector.quantize_mx(
                            out=wq[:, t, lo:hi].bitcast(FP8X4),
                            scales=ws[:, t, lo:hi],
                            in_=wb[:, t, lo:hi, :].rearrange("p m j -> p (m j)"),
                        )
            return wq, ws

        def gather(e, count):
            xgw = work.tile([P, count * C], U32, name="xgw", align_bytes=64)
            xgs = work.tile([P, count * C], U8, name="xgs", align_bytes=64)
            cols = slice(e * C // 16, (e + count) * C // 16)
            nc.vector.tensor_copy(xgw[:], xq[:].bitcast(U32).indirect(offs_t[:, cols]))
            nc.vector.tensor_copy(xgs[:], xs[:].indirect(offs_t[:, cols]))
            return [(xgw[:, i * C : (i + 1) * C], xgs[:, i * C : (i + 1) * C]) for i in range(count)]

        def project(weights, tokens, tag):
            wq, ws = weights
            xgw, xgs = tokens
            banks = []
            for half in range(2):
                acc = psum.tile([P, 4, P], F32, name=tag)
                sl = slice(half * P, (half + 1) * P)
                for t in range(4):
                    nc.tensor.matmul_mx(
                        out=acc[:, t, :],
                        lhsT=wq[:, t, :].bitcast(FP8X4),
                        lhsT_scale=ws[:, t, :],
                        rhs=xgw[:, sl].bitcast(FP8X4),
                        rhs_scale=xgs[:, sl],
                        start=True,
                        stop=True,
                    )
                banks.append(acc)
            return banks

        def prepare_w2(pair):
            w2b = work.tile([P, 2, N, 4], BF16, name="w2b", align_bytes=64)
            w2q = work.tile([P, 2 * N], U32, name="w2q", align_bytes=64)
            w2s = work.tile([P, 2 * N], U8, name="w2s", align_bytes=64)
            for i in range(2):
                turn(nc.scalar.copy if i < W2S[pair] else nc.vector.tensor_copy, w2b[:, i], r2[pair][:, i])
            nc.vector.quantize_mx(
                out=w2q[:].bitcast(FP8X4), scales=w2s[:], in_=w2b[:].rearrange("p e n j -> p (e n j)")
            )
            return [(w2q[:, i * N : (i + 1) * N], w2s[:, i * N : (i + 1) * N]) for i in range(2)]

        def finish(acc, weights, hidden, pieces):
            w2q, w2s = weights
            hq, hs = hidden
            for sl in pieces:
                nc.tensor.matmul_mx(
                    out=acc[:, sl],
                    lhsT=w2q.bitcast(FP8X4),
                    lhsT_scale=w2s,
                    rhs=hq[:, sl].bitcast(FP8X4),
                    rhs_scale=hs[:, sl],
                    start=True,
                    stop=True,
                )

        halves = (slice(0, P), slice(P, C))
        whole = (slice(0, C),)
        hidden = []
        w2qs = {}
        tokens = {}
        tokens[0], tokens[1] = gather(0, 2)
        for e in range(E):
            if e == 1:
                tokens[2], tokens[3] = gather(2, 2)
            banks_a = project(prepare(r1[e], "w1", ((0, P),), (MS1[e],)), tokens[e], "acc_a")
            w3qs = prepare(r3[e], "w3", CUTS3[e], MS3[e])
            gs = []
            for half in range(2):
                g = work.tile([P, P, 4], F32, name="g")
                nc.scalar.activation(out=g[:], in_=banks_a[half][:].rearrange("p t n -> p n t"), func=GELU)
                gs.append(g)
            banks_b = project(w3qs, tokens[e], "acc_b")
            for pair in range(2):
                if W2_AT[pair] == e:
                    w2qs[2 * pair], w2qs[2 * pair + 1] = prepare_w2(pair)
            hb = work.tile([P, C, 4], BF16, name="hb", align_bytes=64)
            hq = work.tile([P, C], U32, name="hq", align_bytes=64)
            hs = work.tile([P, C], U8, name="hs", align_bytes=64)
            for half in range(2):
                nc.vector.tensor_tensor(
                    out=hb[:, halves[half], :], in0=gs[half][:], in1=banks_b[half][:].rearrange("p t n -> p n t"), op=MULT
                )
            pieces = halves if e == E - 1 else whole
            for sl in pieces:
                nc.vector.quantize_mx(
                    out=hq[:, sl].bitcast(FP8X4), scales=hs[:, sl], in_=hb[:, sl, :].rearrange("p n j -> p (n j)")
                )
            hidden.append((hq, hs))
            for group in Y_GROUPS:
                if e == Y_AT[group]:
                    y = psum_y.tile([P, 2 * C], F32, name="y")
                    for i, f in enumerate(group):
                        finish(y[:, i * C : (i + 1) * C], w2qs[f], hidden[f], halves if f == E - 1 else whole)
                    lo = group[0] * C
                    hi = lo + len(group) * C
                    cut = lo + P if e == E - 1 and group == (E - 1,) else hi
                    nc.scalar.copy(out=ys[:, lo:cut], in_=y[:, 0 : cut - lo])
                    if cut < hi:
                        nc.scalar.copy(out=ys[:, cut:hi], in_=y[:, cut - lo : hi - lo])

        cuts = (0, 448, T)
        toks = [slice(cuts[i], cuts[i + 1]) for i in range(2)]
        z1 = keep.tile([P, T], F32, name="z1")
        nc.vector.tensor_tensor(z1[:], ys[:].indirect(pos1_t[:]), gates[0][:], MULT)
        z2 = []
        for i in range(2):
            z2.append(keep.tile([P, cuts[i + 1] - cuts[i]], F32, name=f"z2_{i}"))
            cols = slice(cuts[i] // 16, cuts[i + 1] // 16)
            nc.vector.tensor_tensor(z2[i][:], ys[:].indirect(pos2_t[:, cols]), gates[1][:, toks[i]], MULT)
        for i in range(2):
            total = keep.tile([P, cuts[i + 1] - cuts[i]], F32, name=f"total{i}")
            nc.vector.tensor_tensor(total[:], z1[:, toks[i]], z2[i][:], ADD)
            nc.sync.dma_start(out[:, toks[i]], total[:])
